import numpy as np
import ml_dtypes

BF16 = ml_dtypes.bfloat16


def bf(x):
    return np.asarray(x, np.float32).astype(BF16)


def f32(x):
    return np.asarray(x, np.float32)


def f64(x):
    return np.asarray(x).astype(np.float64)


def striped(idx):
    return np.tile(idx.reshape(-1, 16).T, (8, 1))


def rows(idx, k):
    return np.tile(idx, (k, 1))


def look(tab, idx):
    return np.take_along_axis(f64(tab), rows(idx, len(tab)), axis=1)


K, S, V, N = 256, 2048, 512, 512


def setup_inputs():
    return {"tab": f32(np.random.standard_normal((2, K, S))), "y": f32(1.0 * np.random.standard_normal((K, V))), "offs": striped(np.random.permutation(S)[:N])}


def reference(tab, y, offs):
    idx = offs[:16].T.reshape(-1)
    x = look(tab[0], idx) / (1.0 + np.exp(-look(tab[0], idx))) * f64(y) + look(tab[1], idx)
    return x

@@ -1,0 +1,46 @@
+import concourse.mybir as mybir
+
+F32 = mybir.dt.float32
+U16 = mybir.dt.uint16
+MULT = mybir.AluOpType.mult
+ADD = mybir.AluOpType.add
+SILU = mybir.ActivationFunctionType.Silu
+
+P = 128
+
+
+def tile_lookup_resglu_out_kernel(tc, tab, y, offs, out):
+    nc = tc.nc
+    planes, rows, places = tab.shape
+    n = y.shape[1]
+    blocks = rows // P
+
+    with (
+        tc.tile_pool(name="lists", bufs=1) as lists,
+        tc.tile_pool(name="data", bufs=blocks) as data,
+    ):
+        offsets = lists.tile([P, n // 16], U16, name="offsets")
+        nc.sync.dma_start(offsets[:], offs)
+
+        gates, stream, shifts = [], [], []
+        for b in range(blocks):
+            block = slice(b * P, (b + 1) * P)
+            gate = data.tile([P, places], F32, name="gate")
+            nc.sync.dma_start(gate[:], tab[0, block, :])
+            gates.append(gate)
+            factor = data.tile([P, n], F32, name="factor")
+            nc.sync.dma_start(factor[:], y[block, :])
+            stream.append(factor)
+            shift = data.tile([P, places], F32, name="shift")
+            nc.sync.dma_start(shift[:], tab[1, block, :])
+            shifts.append(shift)
+
+        for b in range(blocks):
+            block = slice(b * P, (b + 1) * P)
+            opened = data.tile([P, n], F32, name="opened")
+            nc.scalar.activation(opened[:], gates[b][:].indirect(offsets[:]), SILU)
+            gated = data.tile([P, n], F32, name="gated")
+            nc.vector.tensor_tensor(gated[:], opened[:], stream[b][:], MULT)
+            x = data.tile([P, n], F32, name="x")
+            nc.vector.tensor_tensor(x[:], shifts[b][:].indirect(offsets[:]), gated[:], ADD)
+            nc.sync.dma_start(out[block, :], x[:])

@@ -7,6 +7,7 @@ ADD = mybir.AluOpType.add
 SILU = mybir.ActivationFunctionType.Silu
 
 P = 128
+PIECES = 2
 
 
 def tile_lookup_resglu_out_kernel(tc, tab, y, offs, out):
@@ -41,6 +42,10 @@ def tile_lookup_resglu_out_kernel(tc, tab, y, offs, out):
             nc.scalar.activation(opened[:], gates[b][:].indirect(offsets[:]), SILU)
             gated = data.tile([P, n], F32, name="gated")
             nc.vector.tensor_tensor(gated[:], opened[:], stream[b][:], MULT)
-            x = data.tile([P, n], F32, name="x")
-            nc.vector.tensor_tensor(x[:], shifts[b][:].indirect(offsets[:]), gated[:], ADD)
-            nc.sync.dma_start(out[block, :], x[:])
+            for piece in range(PIECES):
+                width = n // PIECES
+                cols = slice(piece * width, (piece + 1) * width)
+                entries = slice(cols.start // 16, cols.stop // 16)
+                x = data.tile([P, width], F32, name=f"x{piece}")
+                nc.vector.tensor_tensor(x[:], shifts[b][:].indirect(offsets[:, entries]), gated[:, cols], ADD)
+                nc.sync.dma_start(out[block, cols], x[:])

@@ -7,7 +7,7 @@ ADD = mybir.AluOpType.add
 SILU = mybir.ActivationFunctionType.Silu
 
 P = 128
-PIECES = 2
+PIECES = 4
 
 
 def tile_lookup_resglu_out_kernel(tc, tab, y, offs, out):
@@ -32,8 +32,9 @@ def tile_lookup_resglu_out_kernel(tc, tab, y, offs, out):
             factor = data.tile([P, n], F32, name="factor")
             nc.sync.dma_start(factor[:], y[block, :])
             stream.append(factor)
+        for b in range(blocks):
             shift = data.tile([P, places], F32, name="shift")
-            nc.sync.dma_start(shift[:], tab[1, block, :])
+            nc.sync.dma_start(shift[:], tab[1, b * P : (b + 1) * P, :])
             shifts.append(shift)
 
         for b in range(blocks):

@@ -20,29 +20,25 @@ def tile_lookup_resglu_out_kernel(tc, tab, y, offs, out):
         tc.tile_pool(name="lists", bufs=1) as lists,
         tc.tile_pool(name="data", bufs=blocks) as data,
     ):
+        gates = [data.tile([P, places], F32, name=f"gate{b}") for b in range(blocks)]
+        shifts = [data.tile([P, places], F32, name=f"shift{b}") for b in range(blocks)]
+        stream = data.tile([P, blocks, n], F32, name="stream")
         offsets = lists.tile([P, n // 16], U16, name="offsets")
-        nc.sync.dma_start(offsets[:], offs)
 
-        gates, stream, shifts = [], [], []
+        nc.sync.dma_start(gates[0][:], tab[0, :P, :])
+        nc.sync.dma_start(offsets[:], offs)
+        nc.sync.dma_start(stream[:], y.rearrange("(b p) n -> p b n", p=P))
+        for b in range(1, blocks):
+            nc.sync.dma_start(gates[b][:], tab[0, b * P : (b + 1) * P, :])
         for b in range(blocks):
-            block = slice(b * P, (b + 1) * P)
-            gate = data.tile([P, places], F32, name="gate")
-            nc.sync.dma_start(gate[:], tab[0, block, :])
-            gates.append(gate)
-            factor = data.tile([P, n], F32, name="factor")
-            nc.sync.dma_start(factor[:], y[block, :])
-            stream.append(factor)
-        for b in range(blocks):
-            shift = data.tile([P, places], F32, name="shift")
-            nc.sync.dma_start(shift[:], tab[1, b * P : (b + 1) * P, :])
-            shifts.append(shift)
+            nc.sync.dma_start(shifts[b][:], tab[1, b * P : (b + 1) * P, :])
 
         for b in range(blocks):
             block = slice(b * P, (b + 1) * P)
             opened = data.tile([P, n], F32, name="opened")
             nc.scalar.activation(opened[:], gates[b][:].indirect(offsets[:]), SILU)
             gated = data.tile([P, n], F32, name="gated")
-            nc.vector.tensor_tensor(gated[:], opened[:], stream[b][:], MULT)
+            nc.vector.tensor_tensor(gated[:], opened[:], stream[:, b, :], MULT)
             for piece in range(PIECES):
                 width = n // PIECES
                 cols = slice(piece * width, (piece + 1) * width)

import concourse.mybir as mybir

F32 = mybir.dt.float32
U16 = mybir.dt.uint16
MULT = mybir.AluOpType.mult
ADD = mybir.AluOpType.add
SILU = mybir.ActivationFunctionType.Silu

P = 128
PIECES = 4


def tile_lookup_resglu_out_kernel(tc, tab, y, offs, out):
    nc = tc.nc
    planes, rows, places = tab.shape
    n = y.shape[1]
    blocks = rows // P

    with (
        tc.tile_pool(name="lists", bufs=1) as lists,
        tc.tile_pool(name="data", bufs=blocks) as data,
    ):
        gates = [data.tile([P, places], F32, name=f"gate{b}") for b in range(blocks)]
        shifts = [data.tile([P, places], F32, name=f"shift{b}") for b in range(blocks)]
        stream = data.tile([P, blocks, n], F32, name="stream")
        offsets = lists.tile([P, n // 16], U16, name="offsets")

        nc.sync.dma_start(gates[0][:], tab[0, :P, :])
        nc.sync.dma_start(offsets[:], offs)
        nc.sync.dma_start(stream[:], y.rearrange("(b p) n -> p b n", p=P))
        for b in range(1, blocks):
            nc.sync.dma_start(gates[b][:], tab[0, b * P : (b + 1) * P, :])
        for b in range(blocks):
            nc.sync.dma_start(shifts[b][:], tab[1, b * P : (b + 1) * P, :])

        for b in range(blocks):
            block = slice(b * P, (b + 1) * P)
            opened = data.tile([P, n], F32, name="opened")
            nc.scalar.activation(opened[:], gates[b][:].indirect(offsets[:]), SILU)
            gated = data.tile([P, n], F32, name="gated")
            nc.vector.tensor_tensor(gated[:], opened[:], stream[:, b, :], MULT)
            for piece in range(PIECES):
                width = n // PIECES
                cols = slice(piece * width, (piece + 1) * width)
                entries = slice(cols.start // 16, cols.stop // 16)
                x = data.tile([P, width], F32, name=f"x{piece}")
                nc.vector.tensor_tensor(x[:], shifts[b][:].indirect(offsets[:, entries]), gated[:, cols], ADD)
                nc.sync.dma_start(out[block, cols], x[:])
